import numpy as np, ml_dtypes
CORES = [76,84,92,100,108,116,124]
N = 7
import mx_ref
NC, G = 256, 2
C = np.float32(0.043)
BF = ml_dtypes.bfloat16
def cut(t, i, w=512):
    return t[:, w * i:w * i + w]
def tile(rs):
    return np.stack(rs, axis=2).reshape(128, -1).astype(BF)
def layer(w, X):
    out = []
    for i in range(G):
        for t in range(len(X)):
            p = mx_ref.matmul(mx_ref.quantize(cut(w, len(X) * i + t)), X[t])
            z = p if t == 0 else z + p
        out.append(z)
    return out
def act(Z):
    return [np.maximum(s * z, 0) * C for z in Z for s in (1, -1)]
def pick(b):
    s = np.zeros((128, 128, 4), np.float32)
    s[np.arange(128), np.arange(128), b] = 1.0
    return mx_ref.quantize(s.reshape(128, 512).astype(BF))
def setup_inputs(rng):
    def f(*shape):
        return mx_ref.flush((rng.standard_normal(shape, dtype=np.float32) * np.exp2(rng.integers(-2, 3, shape[:-1] + (1,)))).astype(BF))
    return {"x": f(N, 128, 4 * NC), "w1": f(N, 128, G * 512), "w2": f(N, 128, 512), "a": f(N, 128, G * 512), "b": f(N, 128, N * 4 * NC)}
def setup_inputs_blocks(rng):
    d = setup_inputs(rng)
    for k in ("x", "w1", "w2", "a", "b"): d[k] = mx_ref.spread(d[k], rng, 2)
    return d
def setup_inputs_wide(rng):
    d = setup_inputs(rng)
    for k in ("x", "w1", "w2", "a", "b"): d[k] = mx_ref.flush((d[k].astype(np.float32) * np.exp2(rng.integers(-6, 7, (N, 1, 1))).astype(np.float32)).astype(BF))
    return d
def setup_inputs_zeros(rng):
    d = setup_inputs(rng); v = d["x"].reshape(N, 128, -1, 4).copy()
    v[np.broadcast_to((rng.random((N, 1, v.shape[2], 1)) < 0.33), v.shape)] = 0
    d["x"] = v.reshape(d["x"].shape)
    return d
def reference(x, w1, w2, a, b):
    H = [mx_ref.quantize(tile(act(layer(w1[j], [mx_ref.quantize(x[j])])))) for j in range(N)]
    y = np.zeros((N, 128, N * NC), np.float32)
    for r in range(N):
        qw = mx_ref.quantize(w2[r])
        for j in range(N):
            y[r][:, NC * j:NC * j + NC] = mx_ref.matmul(qw, H[j])
    S = [pick(t) for t in range(4)]
    z = np.zeros((N, 128, NC, 4), np.float32)
    for c in range(N):
        for r in range(N):
            q = mx_ref.quantize(tile(act(layer(a[r], [mx_ref.quantize(cut(b[r], c, 4 * NC))]))))
            p = np.stack([mx_ref.matmul(S[t], q) for t in range(4)], axis=2)
            z[c] = p if r == 0 else z[c] + p
    return {"y": y, "z": z.reshape(N, 128, 4 * NC)}

from concourse.bass import DstId, RemoteDMATransfer
from concourse.mybir import dt, AluOpType, ActivationFunctionType

N = 7
NC = 256
CORES_ALL = 128
CONST = 0.043

SCRATCH = {
    "xb": ("sbuf", [128, 1024], "bfloat16"),
    "w1b": ("sbuf", [128, 1024], "bfloat16"),
    "w2b": ("sbuf", [128, 512], "bfloat16"),
    "ab": ("sbuf", [128, 1024], "bfloat16"),
    "bb": ("sbuf", [128, 7168], "bfloat16"),
    "eye": ("sbuf", [128, 516], "bfloat16"),
    "ht": ("sbuf", [128, 1024], "bfloat16"),
    "gt": ("sbuf", [128, 7168], "bfloat16"),
    "xq": ("sbuf", [128, 256], "float8_e4m3fn_x4"), "xs": ("sbuf", [128, 256], "uint8"),
    "w1q": ("sbuf", [128, 256], "float8_e4m3fn_x4"), "w1s": ("sbuf", [128, 256], "uint8"),
    "w2q": ("sbuf", [128, 128], "float8_e4m3fn_x4"), "w2s": ("sbuf", [128, 128], "uint8"),
    "aq": ("sbuf", [128, 256], "float8_e4m3fn_x4"), "as_": ("sbuf", [128, 256], "uint8"),
    "bq": ("sbuf", [128, 1792], "float8_e4m3fn_x4"), "bs": ("sbuf", [128, 1792], "uint8"),
    "hq": ("sbuf", [128, 256], "float8_e4m3fn_x4"), "hs": ("sbuf", [128, 256], "uint8"),
    "gq": ("sbuf", [128, 1792], "float8_e4m3fn_x4"), "gs": ("sbuf", [128, 1792], "uint8"),
    "sq": ("sbuf", [128, 512], "float8_e4m3fn_x4"), "ss": ("sbuf", [128, 512], "uint8"),
    "hlq": ("sbuf", [128, 1792], "float8_e4m3fn_x4"), "hls": ("sbuf", [128, 1792], "uint8"),
    "glq": ("sbuf", [128, 1792], "float8_e4m3fn_x4"), "gls": ("sbuf", [128, 1792], "uint8"),
    "rq": ("sbuf", [128, 512], "float8_e4m3fn_x4"), "rs": ("sbuf", [128, 512], "uint8"),
    "yb": ("sbuf", [128, 1792], "float32"),
    "zb": ("sbuf", [128, 1024], "float32"),
    "ps": ("psum", [128, 4096], "float32"),
}
SEMAPHORES = (["h%d" % j for j in range(N)] + ["g%d" % j for j in range(N)] + ["rc0", "rs0", "rc1", "rs1", "sent", "stored"]
              + ["e%d" % k for k in range(90)])


def bits(mask):
    return [1 << k for k in range(16) if (mask >> k) & 1]


def part(mask, k, n):
    b = bits(mask)
    w = len(b) // n
    return sum(b[k * w:k * w + w])


def count(mask):
    return len(bits(mask))


def make_plan(i, T, topo):
    me = T.cores[i]
    chip, die = topo.chip(me), topo.die(me)
    others = sorted([j for j in range(N) if j != i], key=lambda j: (i - j) % N)
    same = [j for j in others if topo.same_plane(chip, topo.chip(T.cores[j]))]
    cross = [j for j in others if j not in same]
    cross = [j for j in cross if not topo.mates(chip, topo.chip(T.cores[j]))] + [j for j in cross if topo.mates(chip, topo.chip(T.cores[j]))]
    order = cross + same
    local = [c for c in range(CORES_ALL) if topo.chip(c) == chip and c != me]
    far = T.cores[cross[0]]
    own_ports = [c for c in local if topo.die(c) == die and topo.may_write(c, far)]
    oth_ports = [c for c in local if topo.die(c) != die and topo.may_write(c, far)]
    oth_plain = [c for c in local if topo.die(c) != die and not topo.may_write(c, far)]
    h_relays = [(own_ports[0], order[0:2]), (own_ports[1], order[2:4]), (oth_plain[0], order[4:6])]
    g_relays = {0: (oth_ports[0], 0), 1: (oth_ports[1], 0), 2: (oth_ports[0], 1), 3: (oth_ports[1], 1)}
    return {"order": order, "h_relays": h_relays, "g_relays": g_relays, "me": me}


def dst_id(topo, c):
    rid, pid, _ = topo.addr(c)
    return DstId(rid=rid, pnc=pid)


def codes(buf, k, n=NC):
    return buf[:, k:k + n].bitcast(dt.uint8)


def plane(buf, k, n=NC):
    return buf[:, k:k + n]


def h_mask(src, dests, T, topo):
    m = topo.mask(src, T.cores[dests[0]])
    for d in dests:
        m &= topo.mask(src, T.cores[d])
    return m


def hop_mask(plan, topo):
    m = topo.mask(plan["me"], plan["h_relays"][0][0])
    for c, _ in plan["h_relays"]:
        m &= topo.mask(plan["me"], c)
    return m


def g_hop_mask(plan, k, topo):
    return part(topo.mask(plan["me"], plan["g_relays"][k][0]), k % 2, 2)


def g_last_mask(plan, k, T, topo):
    dest = T.cores[plan["order"][k]]
    if k in plan["g_relays"]:
        return topo.mask(plan["g_relays"][k][0], dest)
    return part(topo.mask(plan["me"], dest), k % 2, 2)


def relay_program(g, core, T, topo):
    for i in range(N):
        if topo.chip(T.cores[i]) != topo.chip(core):
            continue
        plan = make_plan(i, T, topo)
        sent = 0
        for c, dests in plan["h_relays"]:
            if c != core:
                continue
            arrive = count(hop_mask(plan, topo))
            mask = h_mask(core, dests, T, topo)
            for sem, view, src, land in (("rc0", codes, T.rq, T.hlq), ("rs0", plane, T.rs, T.hls)):
                g.wait_ge(T.sem[sem], arrive)
                g.remote_dma_fused([RemoteDMATransfer(
                    dst_ids=[dst_id(topo, T.cores[d]) for d in dests], dma_engine_mask=mask, remote_sem=T.sem["h%d" % i],
                    srcs=[view(src, 0)], dsts=[view(land, NC * i) for _ in dests])], local_sem=T.sem.sent)
                sent += count(mask)
        for k in sorted(plan["g_relays"]):
            c, slot = plan["g_relays"][k]
            if c != core:
                continue
            arrive = count(g_hop_mask(plan, k, topo))
            dest = T.cores[plan["order"][k]]
            mask = g_last_mask(plan, k, T, topo)
            rid, pid, _ = topo.addr(dest)
            for sem, view, src, land in (("rc", codes, T.rq, T.glq), ("rs", plane, T.rs, T.gls)):
                g.wait_ge(T.sem["%s%d" % (sem, slot)], arrive)
                g.remote_dma(view(land, NC * i), view(src, NC * slot), T.sem["g%d" % i], T.sem.sent, pid, rid, mask)
                sent += count(mask)
        if sent:
            g.wait_ge(T.sem.sent, sent)


def rank_program(g, core, T, topo):
    rank = T.rank_of(core)
    if rank is None:
        relay_program(g, core, T, topo)
        return
    plan = make_plan(rank, T, topo)
    plans = [make_plan(j, T, topo) for j in range(N)]
    order = plan["order"] + [rank]
    queue = {"t": g.tensor, "v": g.vector, "s": g.scalar, "y": g.sync, "g": g}
    used = [0]
    seen = set()

    def ev(instr, n=1):
        name = "e%d" % used[0]
        used[0] += 1
        instr.then_inc(T.sem[name], n)
        return (name, n)

    def need(q, *events):
        for name, n in events:
            if (q, name) not in seen:
                seen.add((q, name))
                queue[q].wait_ge(T.sem[name], n)

    def bank(k, n=512):
        return T.ps[:, 512 * k:512 * k + n]

    def mm(out, wq, ws, wk, xq, xs, xk, n, start=True, stop=True):
        return g.tensor.matmul_mx(out, wq[:, 128 * wk:128 * wk + 128], ws[:, 128 * wk:128 * wk + 128],
                                  xq[:, xk:xk + n], xs[:, xk:xk + n], start, stop)

    def act_s(out, src, sign):
        return g.scalar.activation(out, src, ActivationFunctionType.Relu, scale=sign * CONST)

    def act_v(out, src, sign):
        return g.vector.tensor_scalar(out, src, sign * CONST, 0.0, AluOpType.mult, AluOpType.max)

    def load_b(q, k):
        c = order[k]
        return ev(queue[q].dma_start(T.bb[:, 1024 * k:1024 * k + 1024], T.b[:, 1024 * c:1024 * c + 1024]), 16)
    ld_b = {}
    ld_x = ev(g.sync.dma_start(T.xb[:], T.x[:]), 16)
    ld_w1 = ev(g.scalar.dma_start(T.w1b[:], T.w1[:]), 16)
    ld_a = ev(g.scalar.dma_start(T.ab[:], T.a[:]), 16)
    ld_b[0] = load_b("y", 0)
    ld_b[1] = load_b("s", 1)
    ld_b[2] = load_b("y", 2)
    ld_b[3] = load_b("s", 3)
    ld_w2 = ev(g.scalar.dma_start(T.w2b[:], T.w2[:]), 16)
    for k in (4, 5, 6):
        ld_b[k] = load_b("y", k)

    e_one = ev(g.vector.memset(T.eye[:], 1.0))
    need("g", e_one)
    e_eye = ev(g.affine_select(T.eye[:], T.eye[:], [[1, 516]], AluOpType.is_equal, 0.0, -3, -4))
    need("v", e_eye)
    for b in range(4):
        q = g.vector.quantize_mx(T.sq[:, 128 * b:128 * b + 128], T.ss[:, 128 * b:128 * b + 128], T.eye[:, 3 - b:515 - b])
        if b == 3:
            e_s = ev(q)
        else:
            need("t", ev(q))

    need("v", ld_x)
    need("t", ev(g.vector.quantize_mx(T.xq[:], T.xs[:], T.xb[:])))
    need("v", ld_w1)
    need("t", ev(g.vector.quantize_mx(T.w1q[:], T.w1s[:], T.w1b[:])))
    need("v", ld_a)
    e_a = ev(g.vector.quantize_mx(T.aq[:], T.as_[:], T.ab[:]))
    z0 = ev(mm(bank(0, NC), T.w1q, T.w1s, 0, T.xq, T.xs, 0, NC))
    z1 = ev(mm(bank(1, NC), T.w1q, T.w1s, 1, T.xq, T.xs, 0, NC))
    need("s", z0)
    act_done = [ev(act_s(T.ht[:, 0:1024:4], bank(0, NC), 1.0)), ev(act_s(T.ht[:, 1:1024:4], bank(0, NC), -1.0))]
    need("v", z1)
    act_done += [ev(act_v(T.ht[:, 2:1024:4], bank(1, NC), 1.0)), ev(act_v(T.ht[:, 3:1024:4], bank(1, NC), -1.0))]
    h_acts = list(act_done)
    need("v", *act_done)
    e_h = ev(g.vector.quantize_mx(T.hq[:], T.hs[:], T.ht[:]))
    sent = [0]
    need("g", e_h)
    mask = hop_mask(plan, topo)
    for sem, view, src, land in (("rc0", codes, T.hq, T.rq), ("rs0", plane, T.hs, T.rs)):
        g.remote_dma_fused([RemoteDMATransfer(
            dst_ids=[dst_id(topo, c) for c, _ in plan["h_relays"]], dma_engine_mask=mask, remote_sem=T.sem[sem],
            srcs=[view(src, 0)], dsts=[view(land, 0) for _ in plan["h_relays"]])], local_sem=T.sem.sent)
        sent[0] += count(mask)

    groups = [(0, 2), (2, 2), (4, 2), (6, 1)]
    banks = [(4, 5), (6, 7), (4, 5), (2, 3)]
    acts = {}

    def pack_b(p):
        k, m = groups[p]
        need("v", *[ld_b[k + t] for t in range(m)])
        return ev(g.vector.quantize_mx(T.bq[:, NC * k:NC * (k + m)], T.bs[:, NC * k:NC * (k + m)], T.bb[:, 1024 * k:1024 * (k + m)]))

    def products(p, e_b):
        k, m = groups[p]
        need("t", e_a, e_b)
        out = []
        for t in range(2):
            if p == 2:
                need("t", *(acts[0][0:2] if t == 0 else acts[0][2:4]))
            out.append(ev(mm(bank(banks[p][t], NC * m), T.aq, T.as_, t, T.bq, T.bs, NC * k, NC * m)))
        return out

    def steps(p, zs):
        k, m = groups[p]
        b0, b1 = bank(banks[p][0], NC * m), bank(banks[p][1], NC * m)
        col = lambda b: T.gt[:, 1024 * k + b:1024 * (k + m):4]
        need("s", zs[0])
        a0 = ev(act_s(col(0), b0, 1.0))
        a1 = ev(act_s(col(1), b0, -1.0))
        need("v", zs[1])
        a2 = ev(act_v(col(2), b1, 1.0))
        need("s", a2)
        a3 = ev(act_s(col(3), b1, -1.0))
        acts[p] = [a0, a1, a2, a3]

    def pack_g(p):
        k, m = groups[p]
        need("v", *acts[p])
        return ev(g.vector.quantize_mx(T.gq[:, NC * k:NC * (k + m)], T.gs[:, NC * k:NC * (k + m)], T.gt[:, 1024 * k:1024 * (k + m)]))

    def send_g(p, e_g):
        k0, m = groups[p]
        need("g", e_g)
        for what in ("c", "s"):
            view, src = (codes, T.gq) if what == "c" else (plane, T.gs)
            transfers = []
            for k in (k0, k0 + 1):
                if k in plan["g_relays"]:
                    c, slot = plan["g_relays"][k]
                    mk = g_hop_mask(plan, k, topo)
                    sem = "r%s%d" % (what, slot)
                    land = view(T.rq if what == "c" else T.rs, NC * slot)
                else:
                    c = T.cores[plan["order"][k]]
                    mk = g_last_mask(plan, k, T, topo)
                    sem = "g%d" % rank
                    land = view(T.glq if what == "c" else T.gls, NC * rank)
                transfers.append(RemoteDMATransfer(dst_ids=[dst_id(topo, c)], dma_engine_mask=mk, remote_sem=T.sem[sem],
                                                   srcs=[view(src, NC * k)], dsts=[land]))
                sent[0] += count(mk)
            g.remote_dma_fused(transfers, local_sem=T.sem.sent)

    zs = products(0, pack_b(0))
    steps(0, zs)
    zs = products(1, pack_b(1))
    send_g(0, pack_g(0))
    steps(1, zs)
    zs = products(2, pack_b(2))
    send_g(1, pack_g(1))
    steps(2, zs)
    e_b3 = pack_b(3)
    need("v", ld_w2)
    e_w2 = ev(g.vector.quantize_mx(T.w2q[:], T.w2s[:], T.w2b[:]))
    zs = products(3, e_b3)
    send_g(2, pack_g(2))
    steps(3, zs)
    e_own = pack_g(3)

    jobs = []
    for j in range(N):
        if j == rank:
            continue
        kg = plans[j]["order"].index(rank)
        jobs.append(((1.0 if kg < 2 else 2.0 if kg > 3 else 2.1) + 0.01 * kg, "g", j))
        for c, dests in plans[j]["h_relays"]:
            if rank in dests:
                jobs.append((0.9 + 0.2 * dests.index(rank) + 0.001 * j, "h", j))
    jobs = [(0.0, "h", rank), (0.0, "g", rank)] + sorted(jobs)
    last_g = [j for _, kind, j in jobs if kind == "g"][-1]
    ybanks = [6, 7, 4, 5]
    busy = {6: acts[1][0:2], 7: acts[1][2:4], 4: acts[2][0:2], 5: acts[2][2:4]}
    ny = 0
    stored = 0
    done_z = []
    for _, kind, j in jobs:
        if kind == "h":
            if j == rank:
                need("t", e_w2, e_h)
                src, pl, at = T.hq, T.hs, 0
            else:
                for c, dests in plans[j]["h_relays"]:
                    if rank in dests:
                        n = 2 * count(h_mask(c, dests, T, topo))
                need("t", ("h%d" % j, n))
                src, pl, at = T.hlq, T.hls, NC * j
            k = ybanks[ny % 4]
            need("t", *busy[k])
            e = ev(mm(bank(k, NC), T.w2q, T.w2s, 0, src, pl, at, NC))
            out = T.yb[:, NC * j:NC * j + NC]
            if ny % 2 == 0:
                need("s", e)
                e = ev(g.scalar.activation(out, bank(k, NC), ActivationFunctionType.Copy))
            else:
                need("v", e)
                e = ev(g.vector.tensor_copy(out, bank(k, NC)))
            busy[k] = [e]
            need("y", e)
            g.sync.dma_start(T.y[:, NC * j:NC * j + NC], out).then_inc(T.sem.stored, 16)
            stored += 16
            ny += 1
        else:
            if j == rank:
                need("t", e_s, e_own, *h_acts)
                need("t", *acts[3])
                src, pl, at = T.gq, T.gs, NC * 6
            else:
                n = 2 * count(g_last_mask(plans[j], plans[j]["order"].index(rank), T, topo))
                need("t", ("g%d" % j, n))
                src, pl, at = T.glq, T.gls, NC * j
            for b in range(4):
                m = mm(bank(b, NC), T.sq, T.ss, b, src, pl, at, NC, j == rank, j == last_g)
                if j == last_g:
                    done_z.append(ev(m))
    copies = []
    for b in range(4):
        out = T.zb[:, b:1024:4]
        if b % 2 == 0:
            need("v", done_z[b])
            copies.append(ev(g.vector.tensor_copy(out, bank(b, NC))))
        else:
            need("s", done_z[b])
            copies.append(ev(g.scalar.activation(out, bank(b, NC), ActivationFunctionType.Copy)))
    need("y", *copies)
    g.sync.dma_start(T.z[:], T.zb[:]).then_inc(T.sem.stored, 16)
    g.sync.wait_ge(T.sem.stored, stored + 16)
    g.wait_ge(T.sem.sent, sent[0])
